import numpy as np
import ml_dtypes


def mxq(x, axis, fmt="e4m3"):
    dtype, down = {"e4m3": (ml_dtypes.float8_e4m3fn, 7), "e5m2": (ml_dtypes.float8_e5m2, 14)}[fmt]
    v = np.moveaxis(np.asarray(x, np.float32).astype(ml_dtypes.bfloat16).astype(np.float64), axis, -1)
    blocks = v.reshape(v.shape[:-1] + (-1, 32))
    amax = np.abs(blocks).max(-1, keepdims=True)
    byte = np.maximum(np.where(amax > 0, np.frexp(amax)[1] - 1 + 127, 0) - down, 1)
    scale = np.exp2(byte - 127.0)
    codes = (blocks / scale).astype(np.float32).astype(dtype).astype(np.float64)
    return np.moveaxis((codes * scale).reshape(v.shape), -1, axis)


WIDE = False


def mx_kscale(k):
    if not WIDE:
        return np.ones(k)
    levels = np.array([10, -10, 5, -5, 0])
    if k % 512:
        return np.exp2(np.random.permutation(np.resize(levels, k // 32))).repeat(32)
    a = np.empty((k // 512, 16))
    for p in range(k // 512):
        a[p, :8] = np.random.permutation(np.resize(levels, 8))
        for g in range(8):
            far = levels[np.abs(levels - a[p, g]) >= 10]
            a[p, g + 8] = far[np.random.randint(len(far))]
    return np.exp2(a.ravel()).repeat(32)


def f64(x):
    return np.asarray(x).astype(np.float64)


def striped(idx):
    return np.tile(np.asarray(idx).reshape(-1, 16).T, (8, 1)).astype(np.uint16)


def unstriped(offs):
    return offs[:16].T.reshape(-1).astype(np.int64)


E2M1 = np.array([0.0, 0.5, 1.0, 1.5, 2.0, 3.0, 4.0, 6.0, -0.0, -0.5, -1.0, -1.5, -2.0, -3.0, -4.0, -6.0])


def pack_weight(w, fmt):
    k, n = w.shape
    w = f64(np.asarray(w, np.float32).astype(ml_dtypes.bfloat16)).reshape(k // 32, 32, n)
    amax = np.abs(w).max(1)
    if fmt == "e4m3":
        byte = np.frexp(amax)[1] - 1 + 127 - 7
    else:
        mant, ex = np.frexp(amax / 6.0)
        byte = np.where(mant > 0.5, ex, ex - 1) + 127
    byte = np.clip(np.where(amax > 0, byte, 1), 1, 254)
    scaled = (w * np.exp2(127.0 - byte)[:, None, :]).reshape(k, n).astype(np.float32)
    by_word = np.ascontiguousarray(scaled.reshape(k // 512, 128, 4, n).transpose(0, 1, 3, 2))
    if fmt == "e4m3":
        words = by_word.astype(ml_dtypes.float8_e4m3fn).view(np.uint8)
    else:
        c = by_word.astype(ml_dtypes.float4_e2m1fn).view(np.uint8) & 0xF
        words = (c[..., 0::2] | (c[..., 1::2] << 4)).reshape(k // 512, 128, 2 * n)
    return np.ascontiguousarray(words), np.ascontiguousarray(byte.astype(np.uint8).reshape(k // 512, 16, n))


def unpack_weight(words, scales, fmt):
    g, _, n = scales.shape
    words = np.ascontiguousarray(words).reshape(g, 128, n, -1)
    if fmt == "e4m3":
        vals = words.view(ml_dtypes.float8_e4m3fn).astype(np.float64)
    else:
        nib = np.empty((g, 128, n, 4), np.uint8)
        nib[..., 0::2] = words & 0xF
        nib[..., 1::2] = words >> 4
        vals = E2M1[nib]
    vals = vals * np.repeat(np.exp2(scales.astype(np.float64) - 127.0), 8, axis=1)[..., None]
    return vals.transpose(0, 1, 3, 2).reshape(g * 512, n)


def bf(x):
    return np.asarray(x, np.float32).astype(ml_dtypes.bfloat16)


def planes(Y):
    r, m = Y.shape
    b = f64(bf(Y)).reshape(r // 32, 32, m)
    amax = np.abs(b).max(1)
    byte = np.clip(np.where(amax > 0, np.frexp(amax)[1] - 1 + 127 - 7, 1), 1, 254)
    codes = (b * np.exp2(127.0 - byte)[:, None, :]).reshape(r, m).astype(np.float32).astype(ml_dtypes.float8_e4m3fn).view(np.uint8)
    words = codes.reshape(r // 512, 128, 4, m).transpose(0, 1, 3, 2)
    return np.ascontiguousarray(words), np.ascontiguousarray(byte.astype(np.uint8).reshape(r // 512, 16, m))


K, L, M, T, J, N = 512, 512, 512, 512, 1024, 512


def setup_inputs():
    n = np.random.standard_normal
    idx = np.random.randint(0, T, J)
    idx2 = np.random.randint(0, T, J)
    idx3 = np.random.randint(0, T, J)
    fk = mx_kscale(K)
    fl = mx_kscale(L)
    fm = mx_kscale(M)
    bap = pack_weight(n((K, T)) / fk[:, None], "e4m3")
    bbp = pack_weight(n((L, T)) / fl[:, None], "e2m1")
    wbp = pack_weight(n((L, N)) * 1 / np.sqrt(L) * fl[:, None], "e4m3")
    bcp = pack_weight(n((M, T)) / fm[:, None], "e2m1")
    wcp = pack_weight(n((M, N)) * 1 / np.sqrt(M) * fm[:, None], "e4m3")
    return {
        "ba_words": bap[0],
        "ba_scales": bap[1],
        "wa": (n((K, N)) * 1 / np.sqrt(K) * fk[:, None]).astype(np.float32),
        "bb_words": bbp[0],
        "bb_scales": bbp[1],
        "wb_words": wbp[0],
        "wb_scales": wbp[1],
        "bc_words": bcp[0],
        "bc_scales": bcp[1],
        "wc_words": wcp[0],
        "wc_scales": wcp[1],
        "sc1": (np.random.uniform(0.5, 2.0, (1, J))).astype(np.float32),
        "offs": striped(idx),
        "offs2": striped(idx2),
        "offs3": striped(idx3),
    }


def reference(ba_words, ba_scales, wa, bb_words, bb_scales, wb_words, wb_scales, bc_words, bc_scales, wc_words, wc_scales, sc1, offs, offs2, offs3):
    idx = unstriped(offs)
    idx2 = unstriped(offs2)
    idx3 = unstriped(offs3)
    bau = unpack_weight(ba_words, ba_scales, "e4m3")
    bbu = unpack_weight(bb_words, bb_scales, "e2m1")
    wbu = unpack_weight(wb_words, wb_scales, "e4m3")
    bcu = unpack_weight(bc_words, bc_scales, "e2m1")
    wcu = unpack_weight(wc_words, wc_scales, "e4m3")
    waq = mxq(f64(wa), 0, "e4m3")
    za = waq.T @ bau
    zb = wbu.T @ bbu
    zc = wcu.T @ bcu
    y = np.maximum(za[:, idx] + zb[:, idx2] + zc[:, idx3], 0.0) * f64(sc1)
    words, scales = planes(y)
    return y, words, scales

@@ -1,0 +1,193 @@
+from contextlib import ExitStack
+
+import concourse.mybir as mybir
+from concourse.masks import make_identity
+
+F32 = mybir.dt.float32
+BF16 = mybir.dt.bfloat16
+I32 = mybir.dt.int32
+U32 = mybir.dt.uint32
+U16 = mybir.dt.uint16
+U8 = mybir.dt.uint8
+FP8X4 = mybir.dt.float8_e4m3fn_x4
+FP4X4 = mybir.dt.float4_e2m1fn_x4
+ACT = mybir.ActivationFunctionType
+ALU = mybir.AluOpType
+
+P = 128
+PACK = 4
+T = 512
+N = 512
+J = 1024
+SLICES = N // P
+SPARE = 192
+PARTS = ((0, 4), (4, 2), (6, 2))
+
+FLOPS = 3 * 2 * 512 * N * T
+
+
+def tile_list_codes_through_tables_pl_kernel(
+    tc, ba_words, ba_scales, wa, bb_words, bb_scales, wb_words, wb_scales,
+    bc_words, bc_scales, wc_words, wc_scales, sc1, offs, offs2, offs3, out_0, out_1, out_2,
+):
+    nc = tc.nc
+    with ExitStack() as ctx:
+        keep = ctx.enter_context(tc.tile_pool(name="keep", bufs=1))
+        ring = ctx.enter_context(tc.tile_pool(name="ring", bufs=9))
+        psum = ctx.enter_context(tc.psum_pool(name="psum", bufs=1))
+
+        lists = [keep.tile([P, J // 16], U16, name="list%d" % i) for i in range(3)]
+        ident = keep.tile([P, P], F32)
+        make_identity(nc, ident[:])
+
+        def scale_tile(name):
+            plane = keep.tile([P, T], U8, name=name, align_bytes=64)
+            nc.vector.memset(plane[:].bitcast(I32), 0)
+            return plane
+
+        def load_scales(plane, rows):
+            for q in range(4):
+                nc.sync.dma_start(out=plane[32 * q : 32 * q + 4, :].bitcast(I32), in_=rows[0, 4 * q : 4 * q + 4, :].bitcast(I32))
+
+        def load_fp8(name, words):
+            codes = keep.tile([P, T], U32, name=name, align_bytes=64)
+            nc.sync.dma_start(out=codes[:].bitcast(I32), in_=words[0].rearrange("p c r -> p (c r)").bitcast(I32))
+            return codes
+
+        def load_fp4(name, words):
+            codes = keep.tile([P, 2 * T], U8, name=name, align_bytes=64)
+            nc.sync.dma_start(out=codes[:].bitcast(I32), in_=words[0].bitcast(I32))
+            return codes
+
+        ba_s = scale_tile("ba_s")
+        zeros = keep.tile([P, SPARE], F32)
+        nc.vector.memset(zeros[:], 0.0)
+        wb_s, bb_s, wc_s, bc_s = [scale_tile(name) for name in ("wb_s", "bb_s", "wc_s", "bc_s")]
+        tables = [keep.tile([P, SLICES * T + SPARE], F32, name="z%d" % i) for i in range(3)]
+        for z in tables:
+            nc.scalar.activation(z[:, SLICES * T :], zeros[:], ACT.Relu)
+
+        wa_rows = wa.rearrange("(p r) n -> p r n", r=PACK)
+        wa_first = keep.tile([P, PACK, P], F32)
+        nc.sync.dma_start(out=wa_first[:], in_=wa_rows[:, :, :P])
+        ba_c = load_fp8("ba_c", ba_words)
+        load_scales(ba_s, ba_scales)
+        nc.sync.dma_start(lists[0][:], offs)
+        wa_rest = keep.tile([P, PACK, N - P], F32)
+        nc.sync.dma_start(out=wa_rest[:], in_=wa_rows[:, :, P:])
+        wb_c = load_fp8("wb_c", wb_words)
+        bb_c = load_fp4("bb_c", bb_words)
+        load_scales(wb_s, wb_scales)
+        load_scales(bb_s, bb_scales)
+        nc.sync.dma_start(lists[1][:], offs2)
+        wc_c = load_fp8("wc_c", wc_words)
+        bc_c = load_fp4("bc_c", bc_words)
+        load_scales(wc_s, wc_scales)
+        load_scales(bc_s, bc_scales)
+        nc.sync.dma_start(lists[2][:], offs3)
+        slot_scale = keep.tile([P, J // P], F32)
+        with nc.allow_non_contiguous_dma(reason="one scale a partition"):
+            nc.sync.dma_start(out=slot_scale[:], in_=sc1[0].rearrange("(b p) -> p b", p=P))
+
+        made = [(0, s) for s in range(SLICES)] + [(i, s) for s in range(SLICES) for i in (1, 2)]
+
+        def table_slice(i, s, w_codes, w_scales, book, book_scales):
+            bank = psum.tile([P, T], F32, name="z_bank", tag="bank%d" % (made.index((i, s)) % 4))
+            nc.tensor.matmul_mx(out=bank[:], lhsT=w_codes.bitcast(FP8X4), lhsT_scale=w_scales, rhs=book, rhs_scale=book_scales[:], start=True, stop=True)
+            first = (SLICES - 1 - s) * T
+            nc.scalar.copy(tables[i][:, first : first + T], bank[:])
+
+        wa_bf = [keep.tile([P, P, PACK], BF16, name="wa_bf%d" % s, align_bytes=64) for s in range(SLICES)]
+        wa_c = [keep.tile([P, P], U32, name="wa_c%d" % s, align_bytes=64) for s in range(SLICES)]
+        wa_s = [keep.tile([P, P], U8, name="wa_s%d" % s, align_bytes=64) for s in range(SLICES)]
+        for s in range(SLICES):
+            raw = wa_first[:] if s == 0 else wa_rest[:, :, (s - 1) * P : s * P]
+            rounding = nc.vector.tensor_copy if s < 2 else nc.scalar.copy
+            rounding(wa_bf[s][:], raw.rearrange("p r n -> p n r"))
+            nc.vector.quantize_mx(out=wa_c[s][:].bitcast(FP8X4), scales=wa_s[s][:], in_=wa_bf[s][:].rearrange("p n r -> p (n r)"))
+            table_slice(0, s, wa_c[s][:], wa_s[s][:], ba_c[:].bitcast(FP8X4), ba_s)
+        for s in range(SLICES):
+            cols = slice(s * P, (s + 1) * P)
+            table_slice(1, s, wb_c[:, cols], wb_s[:, cols], bb_c[:].bitcast(FP4X4), bb_s)
+            table_slice(2, s, wc_c[:, cols], wc_s[:, cols], bc_c[:].bitcast(FP4X4), bc_s)
+
+        def gather(i, s, block, blocks):
+            count = blocks * P
+            first = (SLICES - 1 - s) * T
+            width = T + SPARE if count >= T else T
+            picked = ring.tile([P, T], F32, name="picked")
+            offsets = lists[i][:, block * P // 16 : (block + blocks) * P // 16]
+            nc.vector.tensor_copy(picked[:, :count], tables[i][:, first : first + width].indirect(offsets))
+            return picked
+
+        clipped = keep.tile([P, J // P, PACK, P], F32)
+        scaled = keep.tile([P, J // P, PACK, P], F32)
+        y_bf = keep.tile([P, J, PACK], BF16, align_bytes=64)
+        y_codes = keep.tile([P, J], U32, align_bytes=64)
+        y_scales = keep.tile([P, J], U8, align_bytes=64)
+        y_rows = out_0.rearrange("(p r) j -> p r j", r=PACK)
+        word_rows = out_1[0].rearrange("p c r -> p (c r)").bitcast(I32)
+        last_block = J // P - 1
+
+        def add_up(s, block, blocks, picks):
+            if block == 0:
+                at = 3 - s % 2
+            elif block == 4:
+                at = 4 + s
+            else:
+                at = 0 if block == last_block else s % 2
+            acc = psum.tile([P, 4, P], F32, name="acc", tag="bank%d" % at)
+            for i in range(3):
+                for b in range(blocks):
+                    nc.tensor.matmul(acc[:, b, :], picks[i][:, b * P : (b + 1) * P], ident[:], is_transpose=True,
+                                     start=(i == 0 and b == 0), stop=(i == 2 and b == blocks - 1))
+            quarter = slice(32 * s, 32 * s + 32)
+            sums = acc[:, :blocks, :].rearrange("j b (q r) -> j b r q", r=PACK)
+            if block == last_block:
+                nc.vector.tensor_scalar(scaled[:, block, :, quarter], sums[:, 0], 0.0, slot_scale[:, block : block + 1], ALU.max, ALU.mult)
+                return
+            nc.scalar.activation(clipped[:, block : block + blocks, :, quarter], sums, ACT.Relu)
+            for b in range(block, block + blocks):
+                nc.scalar.activation(scaled[:, b, :, quarter], clipped[:, b, :, quarter], ACT.Copy, scale=slot_scale[:, b : b + 1])
+
+        def turn_back(b, y_part, at):
+            back = psum.tile([P, PACK, P], F32, name="back", tag="bank%d" % ((b + 4) % 8))
+            for r in range(PACK):
+                nc.tensor.transpose(back[:, r, :], scaled[:, b, r, :], ident[:])
+            pairs = back[:].rearrange("p r j -> p j r")
+            if b == last_block:
+                nc.vector.tensor_copy(y_bf[:, b * P : (b + 1) * P, :], pairs)
+                nc.scalar.copy(y_part[:, :, at * P : (at + 1) * P], back[:])
+            else:
+                nc.scalar.copy(y_part[:, :, at * P : (at + 1) * P], back[:])
+                nc.scalar.copy(y_bf[:, b * P : (b + 1) * P, :], pairs)
+
+        def hand_out(block, blocks, y_part):
+            cols = slice(block * P, (block + blocks) * P)
+            nc.sync.dma_start(out=y_rows[:, :, cols], in_=y_part[:])
+            nc.vector.quantize_mx(out=y_codes[:, cols].bitcast(FP8X4), scales=y_scales[:, cols], in_=y_bf[:, cols, :].rearrange("p j r -> p (j r)"))
+            nc.sync.dma_start(out=word_rows[:, cols], in_=y_codes[:, cols].bitcast(I32))
+
+        for block, blocks in PARTS:
+            if block == 0:
+                early = [gather(0, s, block, blocks) for s in range(SLICES)]
+                for s in range(SLICES):
+                    add_up(s, block, blocks, [early[s], gather(1, s, block, blocks), gather(2, s, block, blocks)])
+            else:
+                split = block + blocks - 1 == last_block
+                for s in range(SLICES - 1 if split else SLICES):
+                    add_up(s, block, blocks, [gather(i, s, block, blocks) for i in range(3)])
+            if block + blocks - 1 == last_block:
+                for b in range(block, block + blocks):
+                    add_up(SLICES - 1, b, 1, [gather(i, SLICES - 1, b, 1) for i in range(3)])
+                    y_part = keep.tile([P, PACK, P], F32, name="y_%d" % b)
+                    turn_back(b, y_part, 0)
+                    hand_out(b, 1, y_part)
+            else:
+                y_part = keep.tile([P, PACK, blocks * P], F32, name="y_%d" % block)
+                for b in range(blocks):
+                    turn_back(block + b, y_part, b)
+                hand_out(block, blocks, y_part)
+        for q in range(4):
+            queue = nc.scalar if q % 2 else nc.sync
+            queue.dma_start(out=out_2[0, 4 * q : 4 * q + 4, :].bitcast(I32), in_=y_scales[32 * q : 32 * q + 4, :].bitcast(I32))

@@ -20,8 +20,15 @@ T = 512
 N = 512
 J = 1024
 SLICES = N // P
-SPARE = 192
-PARTS = ((0, 4), (4, 2), (6, 2))
+SPARE = 512
+PARTS = ((0, 3), (3, 3), (6, 2))
+
+Z_BANKS = ((0, 1, 2, 3), (0, 1, 2, 3), (4, 5, 6, 0))
+ON_VECTOR = 2
+IL_FROM = 6
+RING = 4
+RING_BANKS = (6, 0, 5, 4)
+SLOTS = 8
 
 FLOPS = 3 * 2 * 512 * N * T
 
@@ -33,7 +40,6 @@ def tile_list_codes_through_tables_pl_kernel(
     nc = tc.nc
     with ExitStack() as ctx:
         keep = ctx.enter_context(tc.tile_pool(name="keep", bufs=1))
-        ring = ctx.enter_context(tc.tile_pool(name="ring", bufs=9))
         psum = ctx.enter_context(tc.psum_pool(name="psum", bufs=1))
 
         lists = [keep.tile([P, J // 16], U16, name="list%d" % i) for i in range(3)]
@@ -63,9 +69,16 @@ def tile_list_codes_through_tables_pl_kernel(
         zeros = keep.tile([P, SPARE], F32)
         nc.vector.memset(zeros[:], 0.0)
         wb_s, bb_s, wc_s, bc_s = [scale_tile(name) for name in ("wb_s", "bb_s", "wc_s", "bc_s")]
-        tables = [keep.tile([P, SLICES * T + SPARE], F32, name="z%d" % i) for i in range(3)]
-        for z in tables:
-            nc.scalar.activation(z[:, SLICES * T :], zeros[:], ACT.Relu)
+        za = keep.tile([P, SLICES * T + SPARE], F32)
+        nc.scalar.activation(za[:, SLICES * T :], zeros[:], ACT.Relu)
+        zbc = keep.tile([P, 2 * SLICES * T], F32)
+
+        def place(i, s):
+            if i == 0:
+                return za, (SLICES - 1 - s) * T
+            if i == 1:
+                return zbc, max(2 * s - 1, 0) * T
+            return zbc, min(2 * s + 2, 2 * SLICES - 1) * T
 
         wa_rows = wa.rearrange("(p r) n -> p r n", r=PACK)
         wa_first = keep.tile([P, PACK, P], F32)
@@ -73,35 +86,35 @@ def tile_list_codes_through_tables_pl_kernel(
         ba_c = load_fp8("ba_c", ba_words)
         load_scales(ba_s, ba_scales)
         nc.sync.dma_start(lists[0][:], offs)
-        wa_rest = keep.tile([P, PACK, N - P], F32)
-        nc.sync.dma_start(out=wa_rest[:], in_=wa_rows[:, :, P:])
+        wa_second = keep.tile([P, PACK, P], F32)
+        nc.sync.dma_start(out=wa_second[:], in_=wa_rows[:, :, P : 2 * P])
+        wa_rest = keep.tile([P, PACK, 2 * P], F32)
+        nc.sync.dma_start(out=wa_rest[:], in_=wa_rows[:, :, 2 * P :])
         wb_c = load_fp8("wb_c", wb_words)
         bb_c = load_fp4("bb_c", bb_words)
         load_scales(wb_s, wb_scales)
         load_scales(bb_s, bb_scales)
-        nc.sync.dma_start(lists[1][:], offs2)
         wc_c = load_fp8("wc_c", wc_words)
         bc_c = load_fp4("bc_c", bc_words)
         load_scales(wc_s, wc_scales)
         load_scales(bc_s, bc_scales)
+        nc.sync.dma_start(lists[1][:], offs2)
         nc.sync.dma_start(lists[2][:], offs3)
-        slot_scale = keep.tile([P, J // P], F32)
-        with nc.allow_non_contiguous_dma(reason="one scale a partition"):
-            nc.sync.dma_start(out=slot_scale[:], in_=sc1[0].rearrange("(b p) -> p b", p=P))
-
-        made = [(0, s) for s in range(SLICES)] + [(i, s) for s in range(SLICES) for i in (1, 2)]
+        scale_rows = keep.tile([P, P], F32)
+        nc.gpsimd.memset(scale_rows[:], 0.0)
+        nc.sync.dma_start(out=scale_rows[: J // P, :], in_=sc1[0].rearrange("(b p) -> b p", p=P))
 
         def table_slice(i, s, w_codes, w_scales, book, book_scales):
-            bank = psum.tile([P, T], F32, name="z_bank", tag="bank%d" % (made.index((i, s)) % 4))
+            bank = psum.tile([P, T], F32, name="z_bank", tag="bank%d" % Z_BANKS[i][s])
             nc.tensor.matmul_mx(out=bank[:], lhsT=w_codes.bitcast(FP8X4), lhsT_scale=w_scales, rhs=book, rhs_scale=book_scales[:], start=True, stop=True)
-            first = (SLICES - 1 - s) * T
-            nc.scalar.copy(tables[i][:, first : first + T], bank[:])
+            table, first = place(i, s)
+            nc.scalar.copy(table[:, first : first + T], bank[:])
 
         wa_bf = [keep.tile([P, P, PACK], BF16, name="wa_bf%d" % s, align_bytes=64) for s in range(SLICES)]
         wa_c = [keep.tile([P, P], U32, name="wa_c%d" % s, align_bytes=64) for s in range(SLICES)]
         wa_s = [keep.tile([P, P], U8, name="wa_s%d" % s, align_bytes=64) for s in range(SLICES)]
         for s in range(SLICES):
-            raw = wa_first[:] if s == 0 else wa_rest[:, :, (s - 1) * P : s * P]
+            raw = (wa_first, wa_second)[s][:] if s < 2 else wa_rest[:, :, (s - 2) * P : (s - 1) * P]
             rounding = nc.vector.tensor_copy if s < 2 else nc.scalar.copy
             rounding(wa_bf[s][:], raw.rearrange("p r n -> p n r"))
             nc.vector.quantize_mx(out=wa_c[s][:].bitcast(FP8X4), scales=wa_s[s][:], in_=wa_bf[s][:].rearrange("p n r -> p (n r)"))
@@ -111,16 +124,31 @@ def tile_list_codes_through_tables_pl_kernel(
             table_slice(1, s, wb_c[:, cols], wb_s[:, cols], bb_c[:].bitcast(FP4X4), bb_s)
             table_slice(2, s, wc_c[:, cols], wc_s[:, cols], bc_c[:].bitcast(FP4X4), bc_s)
 
-        def gather(i, s, block, blocks):
+        slot_scale = keep.tile([P, J // P], F32)
+        turned = psum.tile([P, P], F32, name="turned", tag="bank7")
+        nc.tensor.transpose(turned[:], scale_rows[:], ident[:])
+        nc.scalar.copy(slot_scale[:], turned[:, : J // P])
+
+        banks = []
+        slots = []
+
+        def next_bank(name):
+            banks.append(name)
+            return psum.tile([P, 4, P], F32, name=name, tag="bank%d" % RING_BANKS[(len(banks) - 1) % RING])
+
+        def gather(i, s, block, blocks, unit):
             count = blocks * P
-            first = (SLICES - 1 - s) * T
-            width = T + SPARE if count >= T else T
-            picked = ring.tile([P, T], F32, name="picked")
+            table, first = place(i, s)
+            width = T + SPARE if count >= T else T + (16 if i == 1 and s > 0 else 0)
+            if count >= T:
+                picked = keep.tile([P, count], F32, name="early%d" % s)
+            else:
+                slots.append(unit)
+                picked = keep.tile([P, count], F32, name="picked", tag="picked%d" % (len(slots) % SLOTS))
             offsets = lists[i][:, block * P // 16 : (block + blocks) * P // 16]
-            nc.vector.tensor_copy(picked[:, :count], tables[i][:, first : first + width].indirect(offsets))
+            nc.vector.tensor_copy(picked[:, :count], table[:, first : first + width].indirect(offsets))
             return picked
 
-        clipped = keep.tile([P, J // P, PACK, P], F32)
         scaled = keep.tile([P, J // P, PACK, P], F32)
         y_bf = keep.tile([P, J, PACK], BF16, align_bytes=64)
         y_codes = keep.tile([P, J], U32, align_bytes=64)
@@ -129,35 +157,31 @@ def tile_list_codes_through_tables_pl_kernel(
         word_rows = out_1[0].rearrange("p c r -> p (c r)").bitcast(I32)
         last_block = J // P - 1
 
-        def add_up(s, block, blocks, picks):
-            if block == 0:
-                at = 3 - s % 2
-            elif block == 4:
-                at = 4 + s
-            else:
-                at = 0 if block == last_block else s % 2
-            acc = psum.tile([P, 4, P], F32, name="acc", tag="bank%d" % at)
+        def add_up(s, block, blocks, picks, slot, fused):
+            acc = next_bank("acc")
             for i in range(3):
                 for b in range(blocks):
                     nc.tensor.matmul(acc[:, b, :], picks[i][:, b * P : (b + 1) * P], ident[:], is_transpose=True,
                                      start=(i == 0 and b == 0), stop=(i == 2 and b == blocks - 1))
             quarter = slice(32 * s, 32 * s + 32)
             sums = acc[:, :blocks, :].rearrange("j b (q r) -> j b r q", r=PACK)
-            if block == last_block:
-                nc.vector.tensor_scalar(scaled[:, block, :, quarter], sums[:, 0], 0.0, slot_scale[:, block : block + 1], ALU.max, ALU.mult)
+            if fused:
+                for b in range(blocks):
+                    nc.vector.tensor_scalar(scaled[:, block + b, :, quarter], sums[:, b], 0.0, slot_scale[:, block + b : block + b + 1], ALU.max, ALU.mult)
                 return
-            nc.scalar.activation(clipped[:, block : block + blocks, :, quarter], sums, ACT.Relu)
-            for b in range(block, block + blocks):
-                nc.scalar.activation(scaled[:, b, :, quarter], clipped[:, b, :, quarter], ACT.Copy, scale=slot_scale[:, b : b + 1])
+            clipped = keep.tile([P, PACK, blocks * 32], F32, name="clipped", tag="clipped%d" % slot)
+            nc.scalar.activation(clipped[:].rearrange("j r m -> j m r"), acc[:, :blocks, :].rearrange("j b (q r) -> j (b q) r", r=PACK), ACT.Relu)
+            for b in range(blocks):
+                nc.scalar.activation(scaled[:, block + b, :, quarter], clipped[:, :, 32 * b : 32 * b + 32], ACT.Copy, scale=slot_scale[:, block + b : block + b + 1])
 
         def turn_back(b, y_part, at):
-            back = psum.tile([P, PACK, P], F32, name="back", tag="bank%d" % ((b + 4) % 8))
+            back = next_bank("back")
             for r in range(PACK):
                 nc.tensor.transpose(back[:, r, :], scaled[:, b, r, :], ident[:])
             pairs = back[:].rearrange("p r j -> p j r")
-            if b == last_block:
-                nc.vector.tensor_copy(y_bf[:, b * P : (b + 1) * P, :], pairs)
+            if b >= IL_FROM:
                 nc.scalar.copy(y_part[:, :, at * P : (at + 1) * P], back[:])
+                nc.vector.tensor_copy(y_bf[:, b * P : (b + 1) * P, :], y_part[:, :, at * P : (at + 1) * P].rearrange("p r j -> p j r"))
             else:
                 nc.scalar.copy(y_part[:, :, at * P : (at + 1) * P], back[:])
                 nc.scalar.copy(y_bf[:, b * P : (b + 1) * P, :], pairs)
@@ -165,29 +189,31 @@ def tile_list_codes_through_tables_pl_kernel(
         def hand_out(block, blocks, y_part):
             cols = slice(block * P, (block + blocks) * P)
             nc.sync.dma_start(out=y_rows[:, :, cols], in_=y_part[:])
-            nc.vector.quantize_mx(out=y_codes[:, cols].bitcast(FP8X4), scales=y_scales[:, cols], in_=y_bf[:, cols, :].rearrange("p j r -> p (j r)"))
+            for first, count in ((block, 2), (block + 2, 1)) if blocks == 3 else ((block, blocks),):
+                run = slice(first * P, (first + count) * P)
+                nc.vector.quantize_mx(out=y_codes[:, run].bitcast(FP8X4), scales=y_scales[:, run], in_=y_bf[:, run, :].rearrange("p j r -> p (j r)"))
             nc.sync.dma_start(out=word_rows[:, cols], in_=y_codes[:, cols].bitcast(I32))
 
-        for block, blocks in PARTS:
-            if block == 0:
-                early = [gather(0, s, block, blocks) for s in range(SLICES)]
-                for s in range(SLICES):
-                    add_up(s, block, blocks, [early[s], gather(1, s, block, blocks), gather(2, s, block, blocks)])
-            else:
-                split = block + blocks - 1 == last_block
-                for s in range(SLICES - 1 if split else SLICES):
-                    add_up(s, block, blocks, [gather(i, s, block, blocks) for i in range(3)])
-            if block + blocks - 1 == last_block:
-                for b in range(block, block + blocks):
-                    add_up(SLICES - 1, b, 1, [gather(i, SLICES - 1, b, 1) for i in range(3)])
-                    y_part = keep.tile([P, PACK, P], F32, name="y_%d" % b)
-                    turn_back(b, y_part, 0)
-                    hand_out(b, 1, y_part)
-            else:
-                y_part = keep.tile([P, PACK, blocks * P], F32, name="y_%d" % block)
-                for b in range(blocks):
-                    turn_back(block + b, y_part, b)
-                hand_out(block, blocks, y_part)
+        units = [(s, block, blocks) for block, blocks in PARTS for s in range(SLICES)]
+        units[-1:] = [(SLICES - 1, last_block - 1, 1), (SLICES - 1, last_block, 1)]
+        early = [gather(0, s, 0, 6, s) for s in range(SLICES)]
+
+        def finish(block, blocks):
+            y_part = keep.tile([P, PACK, blocks * P], F32, name="y_%d" % block)
+            for b in range(blocks):
+                turn_back(block + b, y_part, b)
+            hand_out(block, blocks, y_part)
+
+        waiting = None
+        for u, (s, block, blocks) in enumerate(units):
+            picks = [early[s][:, block * P :] if block < 6 and i == 0 else gather(i, s, block, blocks, u)[:] for i in range(3)]
+            add_up(s, block, blocks, picks, (u + u // SLICES) % 2, u >= len(units) - ON_VECTOR)
+            if waiting:
+                finish(*waiting)
+                waiting = None
+            if s == SLICES - 1:
+                waiting = (block, blocks)
+        finish(*waiting)
         for q in range(4):
             queue = nc.scalar if q % 2 else nc.sync
             queue.dma_start(out=out_2[0, 4 * q : 4 * q + 4, :].bitcast(I32), in_=y_scales[32 * q : 32 * q + 4, :].bitcast(I32))

@@ -26,7 +26,15 @@ PARTS = ((0, 3), (3, 3), (6, 2))
 Z_BANKS = ((0, 1, 2, 3), (0, 1, 2, 3), (4, 5, 6, 0))
 ON_VECTOR = 2
 IL_FROM = 6
-RING = 4
+RUNS = ((0, 4), (4, 2), (6, 2))
+LATE = ("wide0", "wide1", "wide2", "wide3")
+CAST = 2
+LASTB = (5, 4)
+ON_SCALAR = 6
+GATED = 2
+ACC = {0: (6, 0, 5, 4), 3: (6, 6, 0, 5), 6: (4, 1, 2, 3), 7: (0, 0, 0, 1)}
+BACK = (0, 5, 4, 1, 2, 3, 0, 5)
+ORDER = ((3, 4, 5), (), ())
 RING_BANKS = (6, 0, 5, 4)
 SLOTS = 8
 
@@ -86,10 +94,10 @@ def tile_list_codes_through_tables_pl_kernel(
         ba_c = load_fp8("ba_c", ba_words)
         load_scales(ba_s, ba_scales)
         nc.sync.dma_start(lists[0][:], offs)
-        wa_second = keep.tile([P, PACK, P], F32)
-        nc.sync.dma_start(out=wa_second[:], in_=wa_rows[:, :, P : 2 * P])
-        wa_rest = keep.tile([P, PACK, 2 * P], F32)
-        nc.sync.dma_start(out=wa_rest[:], in_=wa_rows[:, :, 2 * P :])
+        wa_middle = keep.tile([P, PACK, 2 * P], F32)
+        nc.sync.dma_start(out=wa_middle[:], in_=wa_rows[:, :, P : 3 * P])
+        wa_last = keep.tile([P, PACK, P], F32)
+        nc.sync.dma_start(out=wa_last[:], in_=wa_rows[:, :, 3 * P :])
         wb_c = load_fp8("wb_c", wb_words)
         bb_c = load_fp4("bb_c", bb_words)
         load_scales(wb_s, wb_scales)
@@ -114,8 +122,8 @@ def tile_list_codes_through_tables_pl_kernel(
         wa_c = [keep.tile([P, P], U32, name="wa_c%d" % s, align_bytes=64) for s in range(SLICES)]
         wa_s = [keep.tile([P, P], U8, name="wa_s%d" % s, align_bytes=64) for s in range(SLICES)]
         for s in range(SLICES):
-            raw = (wa_first, wa_second)[s][:] if s < 2 else wa_rest[:, :, (s - 2) * P : (s - 1) * P]
-            rounding = nc.vector.tensor_copy if s < 2 else nc.scalar.copy
+            raw = (wa_first[:], wa_middle[:, :, :P], wa_middle[:, :, P:], wa_last[:])[s]
+            rounding = nc.vector.tensor_copy if s < CAST else nc.scalar.copy
             rounding(wa_bf[s][:], raw.rearrange("p r n -> p n r"))
             nc.vector.quantize_mx(out=wa_c[s][:].bitcast(FP8X4), scales=wa_s[s][:], in_=wa_bf[s][:].rearrange("p n r -> p (n r)"))
             table_slice(0, s, wa_c[s][:], wa_s[s][:], ba_c[:].bitcast(FP8X4), ba_s)
@@ -124,79 +132,58 @@ def tile_list_codes_through_tables_pl_kernel(
             table_slice(1, s, wb_c[:, cols], wb_s[:, cols], bb_c[:].bitcast(FP4X4), bb_s)
             table_slice(2, s, wc_c[:, cols], wc_s[:, cols], bc_c[:].bitcast(FP4X4), bc_s)
 
-        slot_scale = keep.tile([P, J // P], F32)
+        slot_scale = keep.tile([P, J // P], F32, tag="scales", align_bytes=64)
         turned = psum.tile([P, P], F32, name="turned", tag="bank7")
         nc.tensor.transpose(turned[:], scale_rows[:], ident[:])
         nc.scalar.copy(slot_scale[:], turned[:, : J // P])
 
-        banks = []
-        slots = []
+        def bank(name, at):
+            return psum.tile([P, 4, P], F32, name=name, tag="bank%d" % at)
 
-        def next_bank(name):
-            banks.append(name)
-            return psum.tile([P, 4, P], F32, name=name, tag="bank%d" % RING_BANKS[(len(banks) - 1) % RING])
-
-        def gather(i, s, block, blocks, unit):
+        def gather(i, s, block, blocks, picked):
             count = blocks * P
             table, first = place(i, s)
             width = T + SPARE if count >= T else T + (16 if i == 1 and s > 0 else 0)
-            if count >= T:
-                picked = keep.tile([P, count], F32, name="early%d" % s)
-            else:
-                slots.append(unit)
-                picked = keep.tile([P, count], F32, name="picked", tag="picked%d" % (len(slots) % SLOTS))
             offsets = lists[i][:, block * P // 16 : (block + blocks) * P // 16]
-            nc.vector.tensor_copy(picked[:, :count], table[:, first : first + width].indirect(offsets))
+            nc.vector.tensor_copy(picked, table[:, first : first + width].indirect(offsets))
             return picked
 
         scaled = keep.tile([P, J // P, PACK, P], F32)
         y_bf = keep.tile([P, J, PACK], BF16, align_bytes=64)
         y_codes = keep.tile([P, J], U32, align_bytes=64)
-        y_scales = keep.tile([P, J], U8, align_bytes=64)
         y_rows = out_0.rearrange("(p r) j -> p r j", r=PACK)
         word_rows = out_1[0].rearrange("p c r -> p (c r)").bitcast(I32)
         last_block = J // P - 1
 
-        def add_up(s, block, blocks, picks, slot, fused):
-            acc = next_bank("acc")
+        def add_up(s, block, blocks, picks, slot):
+            acc = bank("acc", ACC[block][s])
             for i in range(3):
                 for b in range(blocks):
                     nc.tensor.matmul(acc[:, b, :], picks[i][:, b * P : (b + 1) * P], ident[:], is_transpose=True,
                                      start=(i == 0 and b == 0), stop=(i == 2 and b == blocks - 1))
             quarter = slice(32 * s, 32 * s + 32)
-            sums = acc[:, :blocks, :].rearrange("j b (q r) -> j b r q", r=PACK)
-            if fused:
-                for b in range(blocks):
-                    nc.vector.tensor_scalar(scaled[:, block + b, :, quarter], sums[:, b], 0.0, slot_scale[:, block + b : block + b + 1], ALU.max, ALU.mult)
-                return
-            clipped = keep.tile([P, PACK, blocks * 32], F32, name="clipped", tag="clipped%d" % slot)
-            nc.scalar.activation(clipped[:].rearrange("j r m -> j m r"), acc[:, :blocks, :].rearrange("j b (q r) -> j (b q) r", r=PACK), ACT.Relu)
+            sums = acc[:, :blocks, :]
+            few = keep.tile([P, PACK, blocks * 32], F32, name="few", tag="few%d" % slot)
+            nc.scalar.activation(few[:].rearrange("j r (c i) -> j c r i", i=4), sums.rearrange("j b (c i r) -> j (b c) r i", i=4, r=PACK), ACT.Relu)
             for b in range(blocks):
-                nc.scalar.activation(scaled[:, block + b, :, quarter], clipped[:, :, 32 * b : 32 * b + 32], ACT.Copy, scale=slot_scale[:, block + b : block + b + 1])
+                nc.scalar.activation(scaled[:, block + b, :, quarter], few[:, :, 32 * b : 32 * b + 32], ACT.Copy, scale=slot_scale[:, block + b : block + b + 1])
 
         def turn_back(b, y_part, at):
-            back = next_bank("back")
+            back = bank("back", BACK[b])
             for r in range(PACK):
                 nc.tensor.transpose(back[:, r, :], scaled[:, b, r, :], ident[:])
-            pairs = back[:].rearrange("p r j -> p j r")
-            if b >= IL_FROM:
-                nc.scalar.copy(y_part[:, :, at * P : (at + 1) * P], back[:])
-                nc.vector.tensor_copy(y_bf[:, b * P : (b + 1) * P, :], y_part[:, :, at * P : (at + 1) * P].rearrange("p r j -> p j r"))
-            else:
-                nc.scalar.copy(y_part[:, :, at * P : (at + 1) * P], back[:])
-                nc.scalar.copy(y_bf[:, b * P : (b + 1) * P, :], pairs)
+            nc.scalar.copy(y_part[:, :, at * P : (at + 1) * P], back[:])
+            if b < ON_SCALAR or b == 6:
+                nc.scalar.copy(y_bf[:, b * P : (b + 1) * P, :], back[:].rearrange("p r j -> p j r"))
 
         def hand_out(block, blocks, y_part):
             cols = slice(block * P, (block + blocks) * P)
             nc.sync.dma_start(out=y_rows[:, :, cols], in_=y_part[:])
-            for first, count in ((block, 2), (block + 2, 1)) if blocks == 3 else ((block, blocks),):
-                run = slice(first * P, (first + count) * P)
-                nc.vector.quantize_mx(out=y_codes[:, run].bitcast(FP8X4), scales=y_scales[:, run], in_=y_bf[:, run, :].rearrange("p j r -> p (j r)"))
-            nc.sync.dma_start(out=word_rows[:, cols], in_=y_codes[:, cols].bitcast(I32))
 
-        units = [(s, block, blocks) for block, blocks in PARTS for s in range(SLICES)]
-        units[-1:] = [(SLICES - 1, last_block - 1, 1), (SLICES - 1, last_block, 1)]
-        early = [gather(0, s, 0, 6, s) for s in range(SLICES)]
+        def planes(first, count):
+            run = slice(first * P, (first + count) * P)
+            nc.vector.quantize_mx(out=y_codes[:, run].bitcast(FP8X4), scales=y_scales[:, run], in_=y_bf[:, run, :].rearrange("p j r -> p (j r)"))
+            nc.sync.dma_start(out=word_rows[:, run], in_=y_codes[:, run].bitcast(I32))
 
         def finish(block, blocks):
             y_part = keep.tile([P, PACK, blocks * P], F32, name="y_%d" % block)
@@ -204,16 +191,46 @@ def tile_list_codes_through_tables_pl_kernel(
                 turn_back(block + b, y_part, b)
             hand_out(block, blocks, y_part)
 
-        waiting = None
-        for u, (s, block, blocks) in enumerate(units):
-            picks = [early[s][:, block * P :] if block < 6 and i == 0 else gather(i, s, block, blocks, u)[:] for i in range(3)]
-            add_up(s, block, blocks, picks, (u + u // SLICES) % 2, u >= len(units) - ON_VECTOR)
-            if waiting:
-                finish(*waiting)
-                waiting = None
-            if s == SLICES - 1:
-                waiting = (block, blocks)
-        finish(*waiting)
+        early = [keep.tile([P, 6 * P], F32, name="early", tag="wide%d" % s) for s in range(SLICES)]
+        for s in range(SLICES):
+            gather(0, s, 0, 6, early[s][:])
+        for part in range(2):
+            for s in range(SLICES):
+                picks = [early[s][:, 3 * part * P :]]
+                for i in (1, 2):
+                    picked = keep.tile([P, 3 * P], F32, name="picked", tag="picked%d%d" % (s, i))
+                    picks.append(gather(i, s, 3 * part, 3, picked[:]))
+                add_up(s, 3 * part, 3, picks, (s + part) % 2)
+                if part == 1 and s == 0:
+                    finish(0, 3)
+        y_mid = [keep.tile([P, PACK, P], F32, name="y_mid%d" % b) for b in range(3)]
+        for s in range(SLICES - 1):
+            late = keep.tile([P, 6 * P], F32, name="late", tag=LATE[s])
+            add_up(s, 6, 2, [gather(i, s, 6, 2, late[:, 2 * i * P : 2 * (i + 1) * P]) for i in range(3)], s % 2)
+            for b in ORDER[s]:
+                turn_back(b, y_mid[b - 3], 0)
+                nc.sync.dma_start(out=y_rows[:, :, b * P : (b + 1) * P], in_=y_mid[b - 3][:])
+        late = keep.tile([P, 6 * P], F32, name="late", tag=LATE[3])
+        for b in range(2):
+            picks = [gather(i, 3, 6 + b, 1, late[:, (3 * b + i) * P : (3 * b + i + 1) * P]) for i in range(3)]
+            acc = bank("acc", ACC[6 + b][3])
+            for i in range(3):
+                nc.tensor.matmul(acc[:, 0, :], picks[i], ident[:], is_transpose=True, start=(i == 0), stop=(i == 2))
+            nc.vector.tensor_scalar(scaled[:, 6 + b, :, 96:].rearrange("j r (c i) -> j c r i", i=4), acc[:, 0, :].rearrange("j (c i r) -> j c r i", i=4, r=PACK),
+                                    0.0, slot_scale[:, 6 + b : 7 + b], ALU.max, ALU.mult)
+        y_scales = keep.tile([P, J], U8, tag="scales", align_bytes=64)
+        for first, count in RUNS[:-1]:
+            planes(first, count)
+        y_late = [keep.tile([P, PACK, P], F32, name="y_late%d" % b) for b in range(2)]
+        turn_back(6, y_late[0], 0)
+        nc.sync.dma_start(out=y_rows[:, :, 6 * P : 7 * P], in_=y_late[0][:])
+        twin = psum.tile([P, PACK, P], F32, name="twin", tag="bank7")
+        for r in range(PACK):
+            nc.tensor.transpose(twin[:, r, :], scaled[:, last_block, r, :], ident[:])
+        nc.vector.tensor_copy(y_bf[:, last_block * P :, :], twin[:].rearrange("p r j -> p j r"))
+        turn_back(last_block, y_late[1], 0)
+        nc.scalar.dma_start(out=y_rows[:, :, last_block * P :], in_=y_late[1][:])
+        planes(*RUNS[-1])
         for q in range(4):
             queue = nc.scalar if q % 2 else nc.sync
             queue.dma_start(out=out_2[0, 4 * q : 4 * q + 4, :].bitcast(I32), in_=y_scales[32 * q : 32 * q + 4, :].bitcast(I32))

@@ -16,27 +16,24 @@ ALU = mybir.AluOpType
 
 P = 128
 PACK = 4
+LINE = 4
+LIST_ROWS = 16
 T = 512
 N = 512
 J = 1024
 SLICES = N // P
-SPARE = 512
-PARTS = ((0, 3), (3, 3), (6, 2))
+BLOCKS = J // P
+QUARTER = P // SLICES
 
-Z_BANKS = ((0, 1, 2, 3), (0, 1, 2, 3), (4, 5, 6, 0))
-ON_VECTOR = 2
-IL_FROM = 6
-RUNS = ((0, 4), (4, 2), (6, 2))
-LATE = ("wide0", "wide1", "wide2", "wide3")
-CAST = 2
-LASTB = (5, 4)
-ON_SCALAR = 6
-GATED = 2
-ACC = {0: (6, 0, 5, 4), 3: (6, 6, 0, 5), 6: (4, 1, 2, 3), 7: (0, 0, 0, 1)}
-BACK = (0, 5, 4, 1, 2, 3, 0, 5)
-ORDER = ((3, 4, 5), (), ())
-RING_BANKS = (6, 0, 5, 4)
-SLOTS = 8
+WIDE = 3
+LAST_PART = 2 * WIDE
+NARROW = BLOCKS - LAST_PART
+SPARE = T
+ROUNDED_ON_VECTOR = 2
+
+ZC_BANKS = (4, 5, 6, 0)
+RING = ZC_BANKS[2:] + ZC_BANKS[1::-1]
+SIDE_BANK = 7
 
 FLOPS = 3 * 2 * 512 * N * T
 
@@ -50,18 +47,17 @@ def tile_list_codes_through_tables_pl_kernel(
         keep = ctx.enter_context(tc.tile_pool(name="keep", bufs=1))
         psum = ctx.enter_context(tc.psum_pool(name="psum", bufs=1))
 
-        lists = [keep.tile([P, J // 16], U16, name="list%d" % i) for i in range(3)]
+        lists = [keep.tile([P, J // LIST_ROWS], U16, name="list%d" % i) for i in range(3)]
         ident = keep.tile([P, P], F32)
         make_identity(nc, ident[:])
 
-        def scale_tile(name):
+        def load_scales(name, rows):
             plane = keep.tile([P, T], U8, name=name, align_bytes=64)
-            nc.vector.memset(plane[:].bitcast(I32), 0)
-            return plane
-
-        def load_scales(plane, rows):
             for q in range(4):
-                nc.sync.dma_start(out=plane[32 * q : 32 * q + 4, :].bitcast(I32), in_=rows[0, 4 * q : 4 * q + 4, :].bitcast(I32))
+                nc.sync.dma_start(
+                    out=plane[32 * q : 32 * q + 4, :].bitcast(I32), in_=rows[0, 4 * q : 4 * q + 4, :].bitcast(I32)
+                )
+            return plane
 
         def load_fp8(name, words):
             codes = keep.tile([P, T], U32, name=name, align_bytes=64)
@@ -73,11 +69,34 @@ def tile_list_codes_through_tables_pl_kernel(
             nc.sync.dma_start(out=codes[:].bitcast(I32), in_=words[0].bitcast(I32))
             return codes
 
-        ba_s = scale_tile("ba_s")
+        def load_wa(name, first_slice, count):
+            raw = keep.tile([P, PACK, count * P], F32, name=name)
+            cols = slice(first_slice * P, (first_slice + count) * P)
+            nc.sync.dma_start(out=raw[:], in_=wa.rearrange("(p r) n -> p r n", r=PACK)[:, :, cols])
+            return [raw[:, :, c * P : (c + 1) * P] for c in range(count)]
+
+        wa_raw = load_wa("wa_first", 0, 1)
+        ba_s = load_scales("ba_s", ba_scales)
+        ba_c = load_fp8("ba_c", ba_words)
+        nc.sync.dma_start(lists[0][:], offs)
+        wa_raw = wa_raw + load_wa("wa_middle", 1, 2) + load_wa("wa_last", 3, 1)
+        wb_c = load_fp8("wb_c", wb_words)
+        bb_c = load_fp4("bb_c", bb_words)
+        wb_s = load_scales("wb_s", wb_scales)
+        bb_s = load_scales("bb_s", bb_scales)
+        wc_c = load_fp8("wc_c", wc_words)
+        bc_c = load_fp4("bc_c", bc_words)
+        wc_s = load_scales("wc_s", wc_scales)
+        bc_s = load_scales("bc_s", bc_scales)
+        nc.sync.dma_start(lists[1][:], offs2)
+        nc.sync.dma_start(lists[2][:], offs3)
+        sc1_rows = keep.tile([P, P], F32)
+        nc.gpsimd.memset(sc1_rows[:], 0.0)
+        nc.sync.dma_start(out=sc1_rows[:BLOCKS, :], in_=sc1[0].rearrange("(b p) -> b p", p=P))
+
+        za = keep.tile([P, SLICES * T + SPARE], F32)
         zeros = keep.tile([P, SPARE], F32)
         nc.vector.memset(zeros[:], 0.0)
-        wb_s, bb_s, wc_s, bc_s = [scale_tile(name) for name in ("wb_s", "bb_s", "wc_s", "bc_s")]
-        za = keep.tile([P, SLICES * T + SPARE], F32)
         nc.scalar.activation(za[:, SLICES * T :], zeros[:], ACT.Relu)
         zbc = keep.tile([P, 2 * SLICES * T], F32)
 
@@ -88,149 +107,152 @@ def tile_list_codes_through_tables_pl_kernel(
                 return zbc, max(2 * s - 1, 0) * T
             return zbc, min(2 * s + 2, 2 * SLICES - 1) * T
 
-        wa_rows = wa.rearrange("(p r) n -> p r n", r=PACK)
-        wa_first = keep.tile([P, PACK, P], F32)
-        nc.sync.dma_start(out=wa_first[:], in_=wa_rows[:, :, :P])
-        ba_c = load_fp8("ba_c", ba_words)
-        load_scales(ba_s, ba_scales)
-        nc.sync.dma_start(lists[0][:], offs)
-        wa_middle = keep.tile([P, PACK, 2 * P], F32)
-        nc.sync.dma_start(out=wa_middle[:], in_=wa_rows[:, :, P : 3 * P])
-        wa_last = keep.tile([P, PACK, P], F32)
-        nc.sync.dma_start(out=wa_last[:], in_=wa_rows[:, :, 3 * P :])
-        wb_c = load_fp8("wb_c", wb_words)
-        bb_c = load_fp4("bb_c", bb_words)
-        load_scales(wb_s, wb_scales)
-        load_scales(bb_s, bb_scales)
-        wc_c = load_fp8("wc_c", wc_words)
-        bc_c = load_fp4("bc_c", bc_words)
-        load_scales(wc_s, wc_scales)
-        load_scales(bc_s, bc_scales)
-        nc.sync.dma_start(lists[1][:], offs2)
-        nc.sync.dma_start(lists[2][:], offs3)
-        scale_rows = keep.tile([P, P], F32)
-        nc.gpsimd.memset(scale_rows[:], 0.0)
-        nc.sync.dma_start(out=scale_rows[: J // P, :], in_=sc1[0].rearrange("(b p) -> b p", p=P))
+        def bank(name, number):
+            return psum.tile([P, PACK, P], F32, name=name, tag="bank%d" % number)
 
-        def table_slice(i, s, w_codes, w_scales, book, book_scales):
-            bank = psum.tile([P, T], F32, name="z_bank", tag="bank%d" % Z_BANKS[i][s])
-            nc.tensor.matmul_mx(out=bank[:], lhsT=w_codes.bitcast(FP8X4), lhsT_scale=w_scales, rhs=book, rhs_scale=book_scales[:], start=True, stop=True)
+        def make_slice(i, s, number, w_codes, w_scales, book, book_scales):
+            product = bank("product", number)[:].rearrange("p a b -> p (a b)")
+            nc.tensor.matmul_mx(
+                out=product, lhsT=w_codes.bitcast(FP8X4), lhsT_scale=w_scales, rhs=book, rhs_scale=book_scales[:],
+                start=True, stop=True,
+            )
             table, first = place(i, s)
-            nc.scalar.copy(table[:, first : first + T], bank[:])
+            nc.scalar.copy(table[:, first : first + T], product)
 
-        wa_bf = [keep.tile([P, P, PACK], BF16, name="wa_bf%d" % s, align_bytes=64) for s in range(SLICES)]
-        wa_c = [keep.tile([P, P], U32, name="wa_c%d" % s, align_bytes=64) for s in range(SLICES)]
-        wa_s = [keep.tile([P, P], U8, name="wa_s%d" % s, align_bytes=64) for s in range(SLICES)]
         for s in range(SLICES):
-            raw = (wa_first[:], wa_middle[:, :, :P], wa_middle[:, :, P:], wa_last[:])[s]
-            rounding = nc.vector.tensor_copy if s < CAST else nc.scalar.copy
-            rounding(wa_bf[s][:], raw.rearrange("p r n -> p n r"))
-            nc.vector.quantize_mx(out=wa_c[s][:].bitcast(FP8X4), scales=wa_s[s][:], in_=wa_bf[s][:].rearrange("p n r -> p (n r)"))
-            table_slice(0, s, wa_c[s][:], wa_s[s][:], ba_c[:].bitcast(FP8X4), ba_s)
+            wa_bf = keep.tile([P, P, PACK], BF16, name="wa_bf%d" % s, align_bytes=64)
+            wa_c = keep.tile([P, P], U32, name="wa_c%d" % s, align_bytes=64)
+            wa_s = keep.tile([P, P], U8, name="wa_s%d" % s, align_bytes=64)
+            rounding = nc.vector.tensor_copy if s < ROUNDED_ON_VECTOR else nc.scalar.copy
+            rounding(wa_bf[:], wa_raw[s].rearrange("p r n -> p n r"))
+            nc.vector.quantize_mx(
+                out=wa_c[:].bitcast(FP8X4), scales=wa_s[:], in_=wa_bf[:].rearrange("p n r -> p (n r)")
+            )
+            make_slice(0, s, s, wa_c[:], wa_s[:], ba_c[:].bitcast(FP8X4), ba_s)
         for s in range(SLICES):
             cols = slice(s * P, (s + 1) * P)
-            table_slice(1, s, wb_c[:, cols], wb_s[:, cols], bb_c[:].bitcast(FP4X4), bb_s)
-            table_slice(2, s, wc_c[:, cols], wc_s[:, cols], bc_c[:].bitcast(FP4X4), bc_s)
+            make_slice(1, s, s, wb_c[:, cols], wb_s[:, cols], bb_c[:].bitcast(FP4X4), bb_s)
+            make_slice(2, s, ZC_BANKS[s], wc_c[:, cols], wc_s[:, cols], bc_c[:].bitcast(FP4X4), bc_s)
 
-        slot_scale = keep.tile([P, J // P], F32, tag="scales", align_bytes=64)
-        turned = psum.tile([P, P], F32, name="turned", tag="bank7")
-        nc.tensor.transpose(turned[:], scale_rows[:], ident[:])
-        nc.scalar.copy(slot_scale[:], turned[:, : J // P])
+        slot_scale = keep.tile([P, BLOCKS], F32, tag="scales", align_bytes=64)
+        sc1_turned = bank("sc1_turned", SIDE_BANK)
+        nc.tensor.transpose(sc1_turned[:, 0, :], sc1_rows[:], ident[:])
+        nc.scalar.copy(slot_scale[:], sc1_turned[:, 0, :BLOCKS])
 
-        def bank(name, at):
-            return psum.tile([P, 4, P], F32, name=name, tag="bank%d" % at)
-
-        def gather(i, s, block, blocks, picked):
-            count = blocks * P
+        def gather(i, s, block, count, picked):
             table, first = place(i, s)
-            width = T + SPARE if count >= T else T + (16 if i == 1 and s > 0 else 0)
-            offsets = lists[i][:, block * P // 16 : (block + blocks) * P // 16]
+            width = T + SPARE if count * P >= T else T + (LIST_ROWS if i == 1 and s > 0 else 0)
+            offsets = lists[i][:, block * P // LIST_ROWS : (block + count) * P // LIST_ROWS]
             nc.vector.tensor_copy(picked, table[:, first : first + width].indirect(offsets))
             return picked
 
-        scaled = keep.tile([P, J // P, PACK, P], F32)
+        def add_up(number, count, picks):
+            sums = bank("sums", number)
+            for i in range(3):
+                for b in range(count):
+                    nc.tensor.matmul(
+                        sums[:, b, :], picks[i][:, b * P : (b + 1) * P], ident[:], is_transpose=True,
+                        start=(i == 0 and b == 0), stop=(i == 2 and b == count - 1),
+                    )
+            return sums[:, :count, :].rearrange("j b (c i r) -> j (b c) r i", i=LINE, r=PACK)
+
+        def by_lines(sorted_rows):
+            return sorted_rows.rearrange("j r (c i) -> j c r i", i=LINE)
+
+        scaled = keep.tile([P, BLOCKS, PACK, P], F32)
+
+        def clip_and_scale(s, block, count, sums, tag):
+            clipped = keep.tile([P, PACK, count * QUARTER], F32, name="clipped", tag=tag)
+            nc.scalar.activation(by_lines(clipped[:]), sums, ACT.Relu)
+            for b in range(count):
+                nc.scalar.activation(
+                    scaled[:, block + b, :, s * QUARTER : (s + 1) * QUARTER],
+                    clipped[:, :, b * QUARTER : (b + 1) * QUARTER],
+                    ACT.Copy, scale=slot_scale[:, block + b : block + b + 1],
+                )
+
+        def turn_back(b, number):
+            back = bank("back", number)
+            for r in range(PACK):
+                nc.tensor.transpose(back[:, r, :], scaled[:, b, r, :], ident[:])
+            return back
+
         y_bf = keep.tile([P, J, PACK], BF16, align_bytes=64)
         y_codes = keep.tile([P, J], U32, align_bytes=64)
         y_rows = out_0.rearrange("(p r) j -> p r j", r=PACK)
-        word_rows = out_1[0].rearrange("p c r -> p (c r)").bitcast(I32)
-        last_block = J // P - 1
 
-        def add_up(s, block, blocks, picks, slot):
-            acc = bank("acc", ACC[block][s])
-            for i in range(3):
-                for b in range(blocks):
-                    nc.tensor.matmul(acc[:, b, :], picks[i][:, b * P : (b + 1) * P], ident[:], is_transpose=True,
-                                     start=(i == 0 and b == 0), stop=(i == 2 and b == blocks - 1))
-            quarter = slice(32 * s, 32 * s + 32)
-            sums = acc[:, :blocks, :]
-            few = keep.tile([P, PACK, blocks * 32], F32, name="few", tag="few%d" % slot)
-            nc.scalar.activation(few[:].rearrange("j r (c i) -> j c r i", i=4), sums.rearrange("j b (c i r) -> j (b c) r i", i=4, r=PACK), ACT.Relu)
-            for b in range(blocks):
-                nc.scalar.activation(scaled[:, block + b, :, quarter], few[:, :, 32 * b : 32 * b + 32], ACT.Copy, scale=slot_scale[:, block + b : block + b + 1])
+        def empty(b, back, y_block):
+            nc.scalar.copy(y_block, back[:])
+            nc.scalar.copy(y_bf[:, b * P : (b + 1) * P, :], back[:].rearrange("p r j -> p j r"))
 
-        def turn_back(b, y_part, at):
-            back = bank("back", BACK[b])
-            for r in range(PACK):
-                nc.tensor.transpose(back[:, r, :], scaled[:, b, r, :], ident[:])
-            nc.scalar.copy(y_part[:, :, at * P : (at + 1) * P], back[:])
-            if b < ON_SCALAR or b == 6:
-                nc.scalar.copy(y_bf[:, b * P : (b + 1) * P, :], back[:].rearrange("p r j -> p j r"))
+        def finish_block(b, number):
+            y_block = keep.tile([P, PACK, P], F32, name="y_block%d" % b)
+            empty(b, turn_back(b, number), y_block[:])
+            nc.sync.dma_start(out=y_rows[:, :, b * P : (b + 1) * P], in_=y_block[:])
 
-        def hand_out(block, blocks, y_part):
-            cols = slice(block * P, (block + blocks) * P)
-            nc.sync.dma_start(out=y_rows[:, :, cols], in_=y_part[:])
+        turns = []
 
-        def planes(first, count):
-            run = slice(first * P, (first + count) * P)
-            nc.vector.quantize_mx(out=y_codes[:, run].bitcast(FP8X4), scales=y_scales[:, run], in_=y_bf[:, run, :].rearrange("p j r -> p (j r)"))
-            nc.sync.dma_start(out=word_rows[:, run], in_=y_codes[:, run].bitcast(I32))
+        def next_in_ring():
+            turns.append(RING[len(turns) % len(RING)])
+            return turns[-1]
 
-        def finish(block, blocks):
-            y_part = keep.tile([P, PACK, blocks * P], F32, name="y_%d" % block)
-            for b in range(blocks):
-                turn_back(block + b, y_part, b)
-            hand_out(block, blocks, y_part)
-
-        early = [keep.tile([P, 6 * P], F32, name="early", tag="wide%d" % s) for s in range(SLICES)]
+        early = [keep.tile([P, LAST_PART * P], F32, name="early", tag="wide%d" % s) for s in range(SLICES)]
         for s in range(SLICES):
-            gather(0, s, 0, 6, early[s][:])
+            gather(0, s, 0, LAST_PART, early[s][:])
         for part in range(2):
+            block = WIDE * part
             for s in range(SLICES):
-                picks = [early[s][:, 3 * part * P :]]
+                picks = [early[s][:, block * P :]]
                 for i in (1, 2):
-                    picked = keep.tile([P, 3 * P], F32, name="picked", tag="picked%d%d" % (s, i))
-                    picks.append(gather(i, s, 3 * part, 3, picked[:]))
-                add_up(s, 3 * part, 3, picks, (s + part) % 2)
+                    picked = keep.tile([P, WIDE * P], F32, name="picked", tag="picked%d%d" % (s, i))
+                    picks.append(gather(i, s, block, WIDE, picked[:]))
+                clip_and_scale(s, block, WIDE, add_up(next_in_ring(), WIDE, picks), "clipped%d" % ((s + part) % 2))
                 if part == 1 and s == 0:
-                    finish(0, 3)
-        y_mid = [keep.tile([P, PACK, P], F32, name="y_mid%d" % b) for b in range(3)]
+                    y_first = keep.tile([P, PACK, WIDE * P], F32)
+                    for b in range(WIDE):
+                        empty(b, turn_back(b, next_in_ring()), y_first[:, :, b * P : (b + 1) * P])
+                    nc.sync.dma_start(out=y_rows[:, :, : WIDE * P], in_=y_first[:])
+
         for s in range(SLICES - 1):
-            late = keep.tile([P, 6 * P], F32, name="late", tag=LATE[s])
-            add_up(s, 6, 2, [gather(i, s, 6, 2, late[:, 2 * i * P : 2 * (i + 1) * P]) for i in range(3)], s % 2)
-            for b in ORDER[s]:
-                turn_back(b, y_mid[b - 3], 0)
-                nc.sync.dma_start(out=y_rows[:, :, b * P : (b + 1) * P], in_=y_mid[b - 3][:])
-        late = keep.tile([P, 6 * P], F32, name="late", tag=LATE[3])
-        for b in range(2):
-            picks = [gather(i, 3, 6 + b, 1, late[:, (3 * b + i) * P : (3 * b + i + 1) * P]) for i in range(3)]
-            acc = bank("acc", ACC[6 + b][3])
-            for i in range(3):
-                nc.tensor.matmul(acc[:, 0, :], picks[i], ident[:], is_transpose=True, start=(i == 0), stop=(i == 2))
-            nc.vector.tensor_scalar(scaled[:, 6 + b, :, 96:].rearrange("j r (c i) -> j c r i", i=4), acc[:, 0, :].rearrange("j (c i r) -> j c r i", i=4, r=PACK),
-                                    0.0, slot_scale[:, 6 + b : 7 + b], ALU.max, ALU.mult)
+            late = keep.tile([P, 3 * NARROW * P], F32, name="late", tag="wide%d" % s)
+            picks = [gather(i, s, LAST_PART, NARROW, late[:, i * NARROW * P : (i + 1) * NARROW * P]) for i in range(3)]
+            number = next_in_ring() if s == 0 else s
+            clip_and_scale(s, LAST_PART, NARROW, add_up(number, NARROW, picks), "clipped%d" % (s % 2))
+            if s == 0:
+                for b in range(WIDE):
+                    finish_block(WIDE + b, 1 + b)
+        s = SLICES - 1
+        late = keep.tile([P, 3 * NARROW * P], F32, name="late", tag="wide%d" % s)
+        for b, number in enumerate((s, 1)):
+            block = LAST_PART + b
+            picks = [gather(i, s, block, 1, late[:, (3 * b + i) * P : (3 * b + i + 1) * P]) for i in range(3)]
+            nc.vector.tensor_scalar(
+                by_lines(scaled[:, block, :, s * QUARTER :]), add_up(number, 1, picks),
+                0.0, slot_scale[:, block : block + 1], ALU.max, ALU.mult,
+            )
+
         y_scales = keep.tile([P, J], U8, tag="scales", align_bytes=64)
-        for first, count in RUNS[:-1]:
-            planes(first, count)
-        y_late = [keep.tile([P, PACK, P], F32, name="y_late%d" % b) for b in range(2)]
-        turn_back(6, y_late[0], 0)
-        nc.sync.dma_start(out=y_rows[:, :, 6 * P : 7 * P], in_=y_late[0][:])
-        twin = psum.tile([P, PACK, P], F32, name="twin", tag="bank7")
-        for r in range(PACK):
-            nc.tensor.transpose(twin[:, r, :], scaled[:, last_block, r, :], ident[:])
-        nc.vector.tensor_copy(y_bf[:, last_block * P :, :], twin[:].rearrange("p r j -> p j r"))
-        turn_back(last_block, y_late[1], 0)
-        nc.scalar.dma_start(out=y_rows[:, :, last_block * P :], in_=y_late[1][:])
-        planes(*RUNS[-1])
+        word_rows = out_1[0].rearrange("p c r -> p (c r)").bitcast(I32)
+
+        def quantise(block, count):
+            cols = slice(block * P, (block + count) * P)
+            nc.vector.quantize_mx(
+                out=y_codes[:, cols].bitcast(FP8X4), scales=y_scales[:, cols],
+                in_=y_bf[:, cols, :].rearrange("p j r -> p (j r)"),
+            )
+            nc.sync.dma_start(out=word_rows[:, cols], in_=y_codes[:, cols].bitcast(I32))
+
+        quantise(0, 4)
+        quantise(4, 2)
+        finish_block(LAST_PART, RING[1])
+        last = slice((BLOCKS - 1) * P, J)
+        nc.vector.tensor_copy(y_bf[:, last, :], turn_back(BLOCKS - 1, SIDE_BANK)[:].rearrange("p r j -> p j r"))
+        y_last = keep.tile([P, PACK, P], F32)
+        nc.scalar.copy(y_last[:], turn_back(BLOCKS - 1, RING[2])[:])
+        nc.scalar.dma_start(out=y_rows[:, :, last], in_=y_last[:])
+        quantise(LAST_PART, NARROW)
         for q in range(4):
             queue = nc.scalar if q % 2 else nc.sync
-            queue.dma_start(out=out_2[0, 4 * q : 4 * q + 4, :].bitcast(I32), in_=y_scales[32 * q : 32 * q + 4, :].bitcast(I32))
+            queue.dma_start(
+                out=out_2[0, 4 * q : 4 * q + 4, :].bitcast(I32), in_=y_scales[32 * q : 32 * q + 4, :].bitcast(I32)
+            )

from contextlib import ExitStack

import concourse.mybir as mybir
from concourse.masks import make_identity

F32 = mybir.dt.float32
BF16 = mybir.dt.bfloat16
I32 = mybir.dt.int32
U32 = mybir.dt.uint32
U16 = mybir.dt.uint16
U8 = mybir.dt.uint8
FP8X4 = mybir.dt.float8_e4m3fn_x4
FP4X4 = mybir.dt.float4_e2m1fn_x4
ACT = mybir.ActivationFunctionType
ALU = mybir.AluOpType

P = 128
PACK = 4
LINE = 4
LIST_ROWS = 16
T = 512
N = 512
J = 1024
SLICES = N // P
BLOCKS = J // P
QUARTER = P // SLICES

WIDE = 3
LAST_PART = 2 * WIDE
NARROW = BLOCKS - LAST_PART
SPARE = T
ROUNDED_ON_VECTOR = 2

ZC_BANKS = (4, 5, 6, 0)
RING = ZC_BANKS[2:] + ZC_BANKS[1::-1]
SIDE_BANK = 7

FLOPS = 3 * 2 * 512 * N * T


def tile_list_codes_through_tables_pl_kernel(
    tc, ba_words, ba_scales, wa, bb_words, bb_scales, wb_words, wb_scales,
    bc_words, bc_scales, wc_words, wc_scales, sc1, offs, offs2, offs3, out_0, out_1, out_2,
):
    nc = tc.nc
    with ExitStack() as ctx:
        keep = ctx.enter_context(tc.tile_pool(name="keep", bufs=1))
        psum = ctx.enter_context(tc.psum_pool(name="psum", bufs=1))

        lists = [keep.tile([P, J // LIST_ROWS], U16, name="list%d" % i) for i in range(3)]
        ident = keep.tile([P, P], F32)
        make_identity(nc, ident[:])

        def load_scales(name, rows):
            plane = keep.tile([P, T], U8, name=name, align_bytes=64)
            for q in range(4):
                nc.sync.dma_start(
                    out=plane[32 * q : 32 * q + 4, :].bitcast(I32), in_=rows[0, 4 * q : 4 * q + 4, :].bitcast(I32)
                )
            return plane

        def load_fp8(name, words):
            codes = keep.tile([P, T], U32, name=name, align_bytes=64)
            nc.sync.dma_start(out=codes[:].bitcast(I32), in_=words[0].rearrange("p c r -> p (c r)").bitcast(I32))
            return codes

        def load_fp4(name, words):
            codes = keep.tile([P, 2 * T], U8, name=name, align_bytes=64)
            nc.sync.dma_start(out=codes[:].bitcast(I32), in_=words[0].bitcast(I32))
            return codes

        def load_wa(name, first_slice, count):
            raw = keep.tile([P, PACK, count * P], F32, name=name)
            cols = slice(first_slice * P, (first_slice + count) * P)
            nc.sync.dma_start(out=raw[:], in_=wa.rearrange("(p r) n -> p r n", r=PACK)[:, :, cols])
            return [raw[:, :, c * P : (c + 1) * P] for c in range(count)]

        wa_raw = load_wa("wa_first", 0, 1)
        ba_s = load_scales("ba_s", ba_scales)
        ba_c = load_fp8("ba_c", ba_words)
        nc.sync.dma_start(lists[0][:], offs)
        wa_raw = wa_raw + load_wa("wa_middle", 1, 2) + load_wa("wa_last", 3, 1)
        wb_c = load_fp8("wb_c", wb_words)
        bb_c = load_fp4("bb_c", bb_words)
        wb_s = load_scales("wb_s", wb_scales)
        bb_s = load_scales("bb_s", bb_scales)
        wc_c = load_fp8("wc_c", wc_words)
        bc_c = load_fp4("bc_c", bc_words)
        wc_s = load_scales("wc_s", wc_scales)
        bc_s = load_scales("bc_s", bc_scales)
        nc.sync.dma_start(lists[1][:], offs2)
        nc.sync.dma_start(lists[2][:], offs3)
        sc1_rows = keep.tile([P, P], F32)
        nc.gpsimd.memset(sc1_rows[:], 0.0)
        nc.sync.dma_start(out=sc1_rows[:BLOCKS, :], in_=sc1[0].rearrange("(b p) -> b p", p=P))

        za = keep.tile([P, SLICES * T + SPARE], F32)
        zeros = keep.tile([P, SPARE], F32)
        nc.vector.memset(zeros[:], 0.0)
        nc.scalar.activation(za[:, SLICES * T :], zeros[:], ACT.Relu)
        zbc = keep.tile([P, 2 * SLICES * T], F32)

        def place(i, s):
            if i == 0:
                return za, (SLICES - 1 - s) * T
            if i == 1:
                return zbc, max(2 * s - 1, 0) * T
            return zbc, min(2 * s + 2, 2 * SLICES - 1) * T

        def bank(name, number):
            return psum.tile([P, PACK, P], F32, name=name, tag="bank%d" % number)

        def make_slice(i, s, number, w_codes, w_scales, book, book_scales):
            product = bank("product", number)[:].rearrange("p a b -> p (a b)")
            nc.tensor.matmul_mx(
                out=product, lhsT=w_codes.bitcast(FP8X4), lhsT_scale=w_scales, rhs=book, rhs_scale=book_scales[:],
                start=True, stop=True,
            )
            table, first = place(i, s)
            nc.scalar.copy(table[:, first : first + T], product)

        for s in range(SLICES):
            wa_bf = keep.tile([P, P, PACK], BF16, name="wa_bf%d" % s, align_bytes=64)
            wa_c = keep.tile([P, P], U32, name="wa_c%d" % s, align_bytes=64)
            wa_s = keep.tile([P, P], U8, name="wa_s%d" % s, align_bytes=64)
            rounding = nc.vector.tensor_copy if s < ROUNDED_ON_VECTOR else nc.scalar.copy
            rounding(wa_bf[:], wa_raw[s].rearrange("p r n -> p n r"))
            nc.vector.quantize_mx(
                out=wa_c[:].bitcast(FP8X4), scales=wa_s[:], in_=wa_bf[:].rearrange("p n r -> p (n r)")
            )
            make_slice(0, s, s, wa_c[:], wa_s[:], ba_c[:].bitcast(FP8X4), ba_s)
        for s in range(SLICES):
            cols = slice(s * P, (s + 1) * P)
            make_slice(1, s, s, wb_c[:, cols], wb_s[:, cols], bb_c[:].bitcast(FP4X4), bb_s)
            make_slice(2, s, ZC_BANKS[s], wc_c[:, cols], wc_s[:, cols], bc_c[:].bitcast(FP4X4), bc_s)

        slot_scale = keep.tile([P, BLOCKS], F32, tag="scales", align_bytes=64)
        sc1_turned = bank("sc1_turned", SIDE_BANK)
        nc.tensor.transpose(sc1_turned[:, 0, :], sc1_rows[:], ident[:])
        nc.scalar.copy(slot_scale[:], sc1_turned[:, 0, :BLOCKS])

        def gather(i, s, block, count, picked):
            table, first = place(i, s)
            width = T + SPARE if count * P >= T else T + (LIST_ROWS if i == 1 and s > 0 else 0)
            offsets = lists[i][:, block * P // LIST_ROWS : (block + count) * P // LIST_ROWS]
            nc.vector.tensor_copy(picked, table[:, first : first + width].indirect(offsets))
            return picked

        def add_up(number, count, picks):
            sums = bank("sums", number)
            for i in range(3):
                for b in range(count):
                    nc.tensor.matmul(
                        sums[:, b, :], picks[i][:, b * P : (b + 1) * P], ident[:], is_transpose=True,
                        start=(i == 0 and b == 0), stop=(i == 2 and b == count - 1),
                    )
            return sums[:, :count, :].rearrange("j b (c i r) -> j (b c) r i", i=LINE, r=PACK)

        def by_lines(sorted_rows):
            return sorted_rows.rearrange("j r (c i) -> j c r i", i=LINE)

        scaled = keep.tile([P, BLOCKS, PACK, P], F32)

        def clip_and_scale(s, block, count, sums, tag):
            clipped = keep.tile([P, PACK, count * QUARTER], F32, name="clipped", tag=tag)
            nc.scalar.activation(by_lines(clipped[:]), sums, ACT.Relu)
            for b in range(count):
                nc.scalar.activation(
                    scaled[:, block + b, :, s * QUARTER : (s + 1) * QUARTER],
                    clipped[:, :, b * QUARTER : (b + 1) * QUARTER],
                    ACT.Copy, scale=slot_scale[:, block + b : block + b + 1],
                )

        def turn_back(b, number):
            back = bank("back", number)
            for r in range(PACK):
                nc.tensor.transpose(back[:, r, :], scaled[:, b, r, :], ident[:])
            return back

        y_bf = keep.tile([P, J, PACK], BF16, align_bytes=64)
        y_codes = keep.tile([P, J], U32, align_bytes=64)
        y_rows = out_0.rearrange("(p r) j -> p r j", r=PACK)

        def empty(b, back, y_block):
            nc.scalar.copy(y_block, back[:])
            nc.scalar.copy(y_bf[:, b * P : (b + 1) * P, :], back[:].rearrange("p r j -> p j r"))

        def finish_block(b, number):
            y_block = keep.tile([P, PACK, P], F32, name="y_block%d" % b)
            empty(b, turn_back(b, number), y_block[:])
            nc.sync.dma_start(out=y_rows[:, :, b * P : (b + 1) * P], in_=y_block[:])

        turns = []

        def next_in_ring():
            turns.append(RING[len(turns) % len(RING)])
            return turns[-1]

        early = [keep.tile([P, LAST_PART * P], F32, name="early", tag="wide%d" % s) for s in range(SLICES)]
        for s in range(SLICES):
            gather(0, s, 0, LAST_PART, early[s][:])
        for part in range(2):
            block = WIDE * part
            for s in range(SLICES):
                picks = [early[s][:, block * P :]]
                for i in (1, 2):
                    picked = keep.tile([P, WIDE * P], F32, name="picked", tag="picked%d%d" % (s, i))
                    picks.append(gather(i, s, block, WIDE, picked[:]))
                clip_and_scale(s, block, WIDE, add_up(next_in_ring(), WIDE, picks), "clipped%d" % ((s + part) % 2))
                if part == 1 and s == 0:
                    y_first = keep.tile([P, PACK, WIDE * P], F32)
                    for b in range(WIDE):
                        empty(b, turn_back(b, next_in_ring()), y_first[:, :, b * P : (b + 1) * P])
                    nc.sync.dma_start(out=y_rows[:, :, : WIDE * P], in_=y_first[:])

        for s in range(SLICES - 1):
            late = keep.tile([P, 3 * NARROW * P], F32, name="late", tag="wide%d" % s)
            picks = [gather(i, s, LAST_PART, NARROW, late[:, i * NARROW * P : (i + 1) * NARROW * P]) for i in range(3)]
            number = next_in_ring() if s == 0 else s
            clip_and_scale(s, LAST_PART, NARROW, add_up(number, NARROW, picks), "clipped%d" % (s % 2))
            if s == 0:
                for b in range(WIDE):
                    finish_block(WIDE + b, 1 + b)
        s = SLICES - 1
        late = keep.tile([P, 3 * NARROW * P], F32, name="late", tag="wide%d" % s)
        for b, number in enumerate((s, 1)):
            block = LAST_PART + b
            picks = [gather(i, s, block, 1, late[:, (3 * b + i) * P : (3 * b + i + 1) * P]) for i in range(3)]
            nc.vector.tensor_scalar(
                by_lines(scaled[:, block, :, s * QUARTER :]), add_up(number, 1, picks),
                0.0, slot_scale[:, block : block + 1], ALU.max, ALU.mult,
            )

        y_scales = keep.tile([P, J], U8, tag="scales", align_bytes=64)
        word_rows = out_1[0].rearrange("p c r -> p (c r)").bitcast(I32)

        def quantise(block, count):
            cols = slice(block * P, (block + count) * P)
            nc.vector.quantize_mx(
                out=y_codes[:, cols].bitcast(FP8X4), scales=y_scales[:, cols],
                in_=y_bf[:, cols, :].rearrange("p j r -> p (j r)"),
            )
            nc.sync.dma_start(out=word_rows[:, cols], in_=y_codes[:, cols].bitcast(I32))

        quantise(0, 4)
        quantise(4, 2)
        finish_block(LAST_PART, RING[1])
        last = slice((BLOCKS - 1) * P, J)
        nc.vector.tensor_copy(y_bf[:, last, :], turn_back(BLOCKS - 1, SIDE_BANK)[:].rearrange("p r j -> p j r"))
        y_last = keep.tile([P, PACK, P], F32)
        nc.scalar.copy(y_last[:], turn_back(BLOCKS - 1, RING[2])[:])
        nc.scalar.dma_start(out=y_rows[:, :, last], in_=y_last[:])
        quantise(LAST_PART, NARROW)
        for q in range(4):
            queue = nc.scalar if q % 2 else nc.sync
            queue.dma_start(
                out=out_2[0, 4 * q : 4 * q + 4, :].bitcast(I32), in_=y_scales[32 * q : 32 * q + 4, :].bitcast(I32)
            )
